import numpy as np, ml_dtypes
CORES = [8,9,10,11,12,13]
N = 6
BF = ml_dtypes.bfloat16
def gentries(a):
    return np.ascontiguousarray(a.reshape(8, 16, -1).transpose(0, 2, 1)).reshape(8, -1)
def gtable(e):
    e = np.asarray(e); return np.ascontiguousarray(e.reshape(8, -1, 16).transpose(0, 2, 1)).reshape(128, -1).astype(np.int32)
P, L, J, RO, NEED = 1024, 8192, 8, 4, 10
def parts(rng):
    share = rng.choice(np.array([0.03, 0.06, 0.12, 0.25, 0.4]), (N, 8, 1, 1))
    dic = np.where(rng.random((N, 8, 1, L)) < share, rng.integers(0, 6, (N, 8, 16, L), dtype=np.int8), rng.integers(6, 16, (N, 8, 16, L), dtype=np.int8))
    pup = (rng.random((N, 8, 16, P)) * rng.integers(2, 13, (N, 8, 1, P))).astype(np.int8)
    return dic, pup, np.argsort(rng.random((N, 8, P)), axis=-1), rng.integers(0, 4096, (N, 8, 16, 1))
def pack(dic, pup, seat, wt):
    return {"dic": dic.astype(np.float32).reshape(N, 128, L).astype(BF), "pup": pup.astype(np.float32).reshape(N, 128, P).astype(BF),
            "seat": np.stack([gtable(a) for a in seat]), "wt": np.ascontiguousarray(wt.reshape(N, 128, 1)).astype(np.int32)}
def setup_inputs(rng):
    return pack(*parts(rng))
def setup_inputs_spread(rng):
    hard = rng.choice(np.array([0.6, 0.85, 0.97]), (N, 8, 1, 1))
    a = np.where(rng.random((N, 8, 1, L)) < hard, 0.1, rng.choice(np.array([0.5, 1.0, 2.0, 6.0]), (N, 8, 1, L)))
    dic = np.minimum(16 * rng.random((N, 8, 16, L)) ** a, 15).astype(np.int8)
    pup = np.minimum(16 * rng.random((N, 8, 16, P)) ** rng.choice(np.array([0.3, 1.0, 2.0, 4.0, 8.0]), (N, 8, 1, P)), 15).astype(np.int8)
    wt = np.minimum(np.exp2(12 * rng.random((N, 8, 16, 1))) - 1, 4095).astype(np.int64)
    return pack(dic, pup, np.argsort(rng.random((N, 8, P)), axis=-1), wt)
def setup_inputs_ends(rng):
    kind = (7 - np.arange(8)[None, :] + N - 1 - np.arange(N)[:, None]) % 4; k4 = kind[:, :, None, None]
    hard = np.where(rng.random((N, 8, 1, L)) < np.where(k4 == 0, 0.6, 0.96), 0.95, 0.3)
    dic = 15 * (rng.random((N, 8, 16, L)) < hard)
    pup = 15 * (rng.random((N, 8, 16, P)) >= rng.choice(np.array([0.6, 0.9, 0.97, 1.0]), (N, 8, 1, P)))
    wt = 4095 * ((rng.random((N, 8, 16, 1)) < 0.6) | (k4 == 0)); wt[:, :, 0] = 4095; wt[:, :, 15] = np.where(kind == 0, 4095, 0)[:, :, None]
    shut = (k4 == 1) & (np.arange(16)[:, None] >= NEED - 1)
    dic = np.where(shut, 15, dic); pup = np.where(shut, 0, pup)
    half = np.arange(P // 2); z = np.stack([half, P - 1 - half], 1).reshape(-1)
    seat = np.stack([np.stack([np.roll(z[::int(rng.choice(np.array([-1, 1])))], int(rng.integers(0, P))) for g in range(8)]) for r in range(N)])
    for r in range(N):
        for g in range(8):
            a = seat[r, g]; one = a[np.array([0, 2, 5, P - J, P - 1])]
            pup[r, g][:, one] = 0; pup[r, g][0, one] = 1
            if kind[r, g] != 1: pup[r, g][:, a[np.array([4, P - 2])]] = 15
    return pack(dic, pup, seat, wt)
def setup_inputs_corners(rng):
    dic, pup, seat, wt = parts(rng); c = int(rng.integers(0, 8))
    for r in range(N):
        for g in range(8):
            k = (r + g + c) % 8
            if k == 0: dic[r, g] = 0
            if k == 1: pup[r, g] = 0; dic[r, g] = np.maximum(dic[r, g], 1)
            if k == 2: wt[r, g] = 0; dic[r, g][:, 111] = 0
            if k == 3: wt[r, g] = 4095
            if k == 4:
                m = np.where(rng.random(L) < 0.1, NEED, NEED - 1); low = np.argsort(rng.random((16, L)), axis=0) < m
                dic[r, g] = np.where(low, rng.integers(0, 8, (16, L)), 15); pup[r, g] = rng.integers(7, 15, (16, P))
            if k == 5: dic[r, g] = 15 - (rng.random((16, L)) < 0.1); pup[r, g] = 15 - np.where(rng.random((16, P)) < 0.35, 0, rng.integers(1, 4, (16, P)))
            if k == 6: dic[r, g] = 7 + (rng.random((16, L)) < 0.6); pup[r, g] = 7 + (rng.random((16, P)) < 0.2)
            if k == 7:
                dic[r, g] = 8; pup[r, g] = rng.integers(0, 3, (16, P)); e = seat[r, g][J - 1::J]
                pup[r, g][:, e] = rng.integers(8, 16, (16, P // J))
    return pack(dic, pup, seat, wt)
def wn(a, b, j=0, t=0):
    return ((a * b >> 5) + 37 * j + 11 * t) & (L - 1)
def hexed(rng, three, kk, lo, hi):
    x = rng.integers(lo, hi + 1, (16, P)); x[three] = (kk[None, :] >> np.array([[0], [4], [8]])) & 15
    return x
def rule(rng, three, hard):
    d = np.where(hard, 15, rng.integers(0, 6, (16, L))); d[three] = rng.integers(0, 16, (3, L))
    return d
def setup_inputs_full(rng):
    dic, pup, seat, wt = parts(rng); c = int(rng.integers(0, 8)); S = P // J
    K = np.arange(4096); V = (K * K >> 5) & (P - 1); W0 = wn(K, K); top = int(V[4095]); z = P - J + 1; every = np.arange(L)
    for g in range(8):
        k = (g + c) % 8; three = rng.permutation(16)[:3]; rest = np.setdiff1d(np.arange(16), three)
        if k < 5: wt[:, g] = 0; wt[:, g, three, 0] = np.array([1, 16, 256])
        if k < 4:
            h1 = wn(4095, 4094)
            sp = int(rng.choice(np.flatnonzero((z - V >= 0) & (z - V < J) & (W0 != h1) & (W0 != wn(4094, 4094))))); jz = z - int(V[sp])
            hs = np.array([h1, int(W0[sp])]); own = K[~np.isin(W0, hs)]; line = {}
            for r in range(N):
                if r % 2 == k % 2: continue
                kk = rng.choice(own, P); kk[top] = 4094; kk[P - 1] = sp
                kk[top + 1] = rng.choice(own[~np.isin(wn(4095, own, 1), hs)]); kk[0] = rng.choice(own[~np.isin(wn(181, own, 1), hs)])
                line[r] = kk; pup[r, g][:, seat[r, g]] = hexed(rng, three, kk, 6, 14); dic[r, g] = rule(rng, three, np.isin(every, hs))
            for r in range(N):
                if r % 2 != k % 2: continue
                kb = line[(r + 1) % N]
                s = K[~np.isin(V, np.array([0, P - 1, top, top + 1])) & ~np.isin(wn(K, kb[V]), hs) & (wn(sp, K, jz) != W0)]
                s = rng.permutation(s); s = rng.permutation(s[np.unique(V[s], return_index=True)[1]])
                more = [4095]
                if k >= 2: more = more + [181, int(rng.choice(np.flatnonzero((V == 0) & ~np.isin(wn(K, kb[0]), hs))))]
                kk = rng.integers(0, 4096, P); kk[0] = 4095
                kk[1::J] = np.concatenate([rng.permutation(np.concatenate([np.array(more), s[:S - 1 - len(more)]])), s[-1:]])
                x = hexed(rng, three, kk, 0, 13); x[:, 0] = 15; x[rest, z] = 14
                d = rule(rng, three, every >= 0); d[rest, wn(sp, int(kk[z]), jz)] = 14
                pup[r, g][:, seat[r, g]] = x; dic[r, g] = d
        if k == 4:
            sa = int(rng.choice(np.flatnonzero(V == P - 1))); ha = int(wn(sa, sa, 0, 1))
            sb = int(rng.choice(np.flatnonzero((K >= 64) & (V < P - J) & (W0 != W0[sa])))); hb = int(W0[sb]); u = int(V[sb])
            own = K[~np.isin(W0, np.array([ha, hb, ha - 11, hb - 11]) & (L - 1))]
            au = own[~np.isin(wn(sb, own), np.array([ha, hb])) & (wn(sa, own, 0, 1) != hb)]
            for r in range(N):
                kk = rng.choice(own, P); kk[u] = rng.choice(au); kk[P - 1] = sa if r < 2 else sb
                pup[r, g][:, seat[r, g]] = hexed(rng, three, kk, 6, 14); dic[r, g] = rule(rng, three, every == (ha if r < 2 else hb))
        if k == 5:
            for r in range(N):
                dic[r, g] = rng.integers(6, 12, (16, L))
                pup[r, g][:, seat[r, g]] = np.where((np.arange(P) + r) % 2 == 0, rng.integers(0, 6, (16, P)), rng.integers(12, 15, (16, P)))
        if k >= 6:
            wt[:, g] = rng.integers(4090, 4096, (N, 16, 1)) if k == 6 else 4095
            for r in range(N):
                x = 13 + (rng.random((16, P)) < 0.7) + (rng.random((16, P)) < 0.15)
                x = np.minimum(x, 15); x[:, np.array([P // 2, P - 1])] = 15
                pup[r, g][:, seat[r, g]] = x
                dic[r, g] = np.where(rng.random(L) < (0.7 if k == 6 else 0.9), 15, rng.integers(0, 14, (16, L)))
    return pack(dic, pup, seat, wt)
def check_inputs(d):
    bad = []
    for k, lo, hi in (("dic", 0, 15), ("pup", 0, 15), ("seat", 0, P - 1), ("wt", 0, 4095)):
        a = np.asarray(d[k]).astype(np.float64)
        if not (np.all(a >= lo) and np.all(a <= hi)): bad.append("range of " + k)
        elif not np.all(a == np.floor(a)): bad.append("whole numbers of " + k)
    for a in d["seat"]:
        if not np.all(np.sort(gentries(np.asarray(a)), axis=1) == np.arange(P)):
            bad.append("permutation of seat"); break
    return bad
def keys(x, o, w):
    xo = np.take_along_axis(x, o[:, None, :], 2)
    return xo, np.add.reduce(xo.astype(np.int64) * w, axis=1) & 4095
def reference(dic, pup, seat, wt):
    d = dic.astype(np.float32).astype(np.int16).reshape(N, 8, 16, L); x = pup.astype(np.float32).astype(np.int16).reshape(N, 8, 16, P)
    o = np.stack([gentries(a) for a in seat]).astype(np.int64); w = wt.astype(np.int64).reshape(N, 8, 16, 1)
    q = np.arange(P); jj = np.arange(J); pl = q[:, None] + jj; inside = pl < P; pc = np.minimum(pl, P - 1)
    for t in range(RO):
        away = []
        for r in range(N):
            xo, s = keys(x[r], o[r], w[r])
            ix = (((s[:, :, None] * s[:, pc]) >> 5) + 37 * jj + 11 * t) & (L - 1)
            D = np.take_along_axis(d[r], ix.reshape(8, 1, -1), 2)
            ok = inside & (np.add.reduce((xo[:, :, pc] >= D.reshape(8, 16, P, J)).astype(np.int16), axis=1) >= NEED)
            found = np.any(ok, axis=2); last = np.where(found, q + np.argmax(ok, axis=2), np.minimum(q + J - 1, P - 1))
            st = np.zeros((8, P), np.int64)
            for g in range(8):
                f = last[g].tolist(); p = 0
                while p < P:
                    st[g, p:f[p] + 1] = p; p = f[p] + 1
            fs = np.take_along_axis(found, st, 1); ls = np.take_along_axis(last, st, 1)
            D2 = np.take_along_axis(D, (st * J + q - st)[:, None, :], 2)
            xo = xo + ((fs & (q < ls))[:, None, :] & (D2 > xo))
            x[r] = np.take_along_axis(xo, np.argsort(o[r], axis=1)[:, None, :], 2)
            o[r] = np.take_along_axis(o[r], np.where(fs, np.where(q == st, ls, q - 1), q), 1)
            away.append((q == st) & ~fs)
        now = [keys(x[r], o[r], w[r]) for r in range(N)]; x0 = x.copy()
        for a in range(N):
            b = (a + 1 + t % (N - 1)) % N; xb, sb = now[b]
            for g in range(8):
                ps = np.flatnonzero(away[a][g])
                if len(ps) == 0: continue
                sv = now[a][1][g, ps]
                v = ((((sv * sv) >> 5) & (P - 1))[:, None] + jj) & (P - 1)
                D = d[b, g][:, (((sv[:, None] * sb[g, v]) >> 5) + 37 * jj + 11 * t) & (L - 1)]
                ok = (np.add.reduce((xb[g][:, v] >= D).astype(np.int16), axis=0) >= NEED) & ~away[b][g, v]
                h = np.flatnonzero(np.any(ok, axis=1))
                if len(h) == 0: continue
                u, i = np.unique(v[h, np.argmax(ok[h], axis=1)], return_index=True)
                pa = o[a][g, ps[h[i]]]; pb = o[b][g, u]
                x[a, g][:, pa] = x0[b, g][:, pb]; x[b, g][:, pb] = x0[a, g][:, pa]
    return {"ypup": x.reshape(N, 128, P).astype(np.float32).astype(BF), "yseat": o.astype(np.float32)}

import numpy as np
from concourse.bass import DstId, RemoteDMATransfer
from concourse.mybir import AluOpType as A, ActivationFunctionType as F

N, RO = 6, 4
KEY16 = True
NS = 7
XW, DUM, NEG, LAND = 1568, 1168, 1296, 1312
OFF = 16384.0
f32, bf, i32, u16 = "float32", "bfloat16", "int32", "uint16"
WD = "float16" if KEY16 else bf

def _b(d, *sh):
    return ("sbuf", [128] + list(sh), d)

SCRATCH = {
    "D": _b(bf, 8496), "LT": _b(bf, 9216), "X0": _b(bf, XW), "X1": _b(bf, XW), "PU": _b(bf, 1024), "Y": _b(bf, DUM + 128),
    "O0": _b(f32, 1168), "O1": _b(f32, 1168), "IO": _b(f32, 1024), "DG": _b(bf, 1536), "LG": _b(bf, 1024), "XV": _b(bf, 1024),
    "L2": _b(bf, 1024), "NQ": _b(bf, 1024), "FM": _b(bf, 1024), "ONE": _b(bf, 1024),
    "SE": _b(i32, 64), "SEU": _b(u16, 64), "WI": _b(i32, 1), "CI": _b(i32, 8), "CF": _b(f32, 32),
    "C0": _b(bf, 144), "C1": _b(bf, 144), "W0": _b(WD, 144), "W1": _b(WD, 144), "W2": _b(WD, 144), "W3": _b(WD, 144), "CQ": _b(f32, 144),
    "ID": _b(bf, 128), "NI": _b(bf, 128), "SH": _b(f32, 128), "BO": _b(f32, 128), "MK": _b(f32, 128), "MS": _b(f32, 16),
    "T1": _b(f32, 512), "T2": _b(f32, 512), "TI": _b(i32, 128), "PIL": _b(u16, 74), "LS": _b(u16, 64),
    "THR": _b(f32, 512), "TH7": _b(f32, 64), "FL": _b(bf, 1024), "EB": _b(f32, 2944), "LM": _b(f32, 184),
    "TB": _b(f32, 560), "KC": _b(f32, 128), "KD": _b(f32, 64), "M1": _b(f32, 128), "E1": _b(f32, 128), "WT": _b(f32, 64), "FT": _b(f32, 64),
    "U": _b(u16, 32 * 15), "G": _b(f32, 16 * 16), "RB": _b(f32, 64), "PW": _b(f32, 80), "B1": _b(f32, 80), "B2": _b(i32, 80), "ST": _b(i32, 80),
    "K0": _b(i32, 72), "KI": _b(i32, 72), "PR": _b(i32, 512), "PS": _b(i32, 512), "IX": _b(u16, 512),
    "JS": _b(bf, 512), "F7": _b(f32, 64), "UN": _b(f32, 64), "S1": _b(f32, 64), "S2": _b(f32, 64), "A2": _b(f32, 72), "BB": _b(f32, 64),
    "C3": _b(f32, 64), "UA": _b(f32, 64), "UX": _b(f32, 64), "NB": _b(f32, 64), "CR": _b(f32, 64), "DMC": _b(f32, 64), "DM8": _b(f32, 8),
    "KP": _b(f32, 64), "KM": _b(f32, 72), "P1": _b(f32, 72), "YS": _b(f32, 72), "P2": _b(f32, 64), "P3": _b(f32, 64), "SV": _b(f32, 64),
    "M16": _b(f32, 64), "SR": _b(f32, 64), "NL": _b(u16, 64), "SL": _b(u16, 64), "AI": _b(i32, 8), "AF": _b(f32, 8), "AWL": _b(u16, 8),
    "SND": _b(i32, RO, 8), "RCV": _b(i32, RO * 8), "VS": _b(bf, RO * 128), "VL": _b(bf, RO * 128), "RS": _b(bf, RO * 128), "RL": _b(bf, RO * 128),
    "HS": _b(i32, 8), "HP": _b(i32, 8), "HA": _b(i32, 8), "HB": _b(i32, 8), "HC": _b(i32, 8), "RAW": _b(i32, 64), "VLS": _b(u16, 64),
    "J16": _b(f32, 64), "J37": _b(f32, 64), "H1": _b(i32, 64), "H2": _b(f32, 64), "H3": _b(f32, 64), "CC": _b(f32, 72), "CD": _b(f32, 128),
    "FH": _b(f32, 128), "THV": _b(f32, 64), "CH": _b(f32, 128), "NCH": _b(f32, 8), "CRL": _b(f32, 8), "DL": _b(f32, 16), "AC": _b(f32, 8),
    "K2": _b(i32, 64), "K3": _b(i32, 64), "K4": _b(i32, 64), "IX2": _b(u16, 64), "ME": _b(f32, 128), "WN": _b(f32, 8), "CHL": _b(u16, 8),
    "OF": _b(f32, 64), "OL": _b(u16, 64), "OA": _b(u16, 8),
    "PZ0": ("psum", [128, 512], f32), "PZ1": ("psum", [128, 512], f32), "PZ2": ("psum", [128, 512], f32), "PC": ("psum", [128, 512], f32),
    "PK": ("psum", [128, 512], f32), "PV": ("psum", [128, 512], f32), "PA": ("psum", [128, 512], f32), "PB": ("psum", [128, 512], f32),
}
SAME = {"H2": "S2", "H3": "S1", "F7": "S2", "M16": "S1", "TI": "PR", "T1": "P1", "SEU": "NL", "W2": "W0", "W3": "W1",
        "TH7": "S1", "SV": "S1", "CQ": "OH", "HP": "HA", "HB": "HA"}
SCRATCH.update({"THR": _b(f32, 72), "ONE": _b(bf, 512), "BIG": _b(bf, 1024), "SND": _b(f32, RO * 64), "RCV": _b(f32, RO * 64),
                "HV": _b(f32, 8), "ME": _b(WD, 128), "BO": _b(WD, 128), "HC": _b(f32, 8), "OH": _b(WD, 1024), "F2": _b(f32, 128),
                "C3": _b(f32, 128), "P3": _b(f32, 128), "KP": _b(f32, 128), "SND": _b(f32, RO * 128), "RCV": _b(f32, RO * 128), "LS": _b(u16, 72)})
SCRATCH = {n: s for n, s in SCRATCH.items() if n not in SAME}
NDMA = 12
SEMAPHORES = ["cG", "cV", "cS", "cP"] + ["d%d" % i for i in range(NDMA)] + ["%s%s%d" % (a, k, t) for a in "al" for k in "kvr" for t in range(RO)]
SHAPES = {n: s[1] for n, s in SCRATCH.items()}
_IDX = {n: np.arange(int(np.prod(s[1:]))).reshape(s[1:]) for n, s in SHAPES.items()}


def order_calls(g, T, ops):
    q = {"G": g, "V": g.vector, "S": g.scalar, "P": g.tensor, "Y": g.sync}
    lastw = {n: np.full(a.size, -1) for n, a in _IDX.items()}
    lastr = {n: {} for n in _IDX}
    bank = {}
    known = {e: {} for e in q}
    waits, clock, pos, cnt, need = [], [], [], {}, set()
    for i, (e, fn, rd, wr, own) in enumerate(ops):
        key = own[0] if own else e
        deps = set()
        for n, el in rd:
            deps.update(np.unique(lastw[n][el]).tolist())
        for n, el in wr:
            deps.update(np.unique(lastw[n][el]).tolist())
            for a in lastr[n].values():
                deps.update(np.unique(a[el]).tolist())
        for n, el in rd + wr:
            if SCRATCH[n][0] == "psum":
                deps.update(j for k, j in bank.get(n, {}).items() if k != e)
        deps.discard(-1)
        best = {}
        for d in deps:
            k, p = pos[d]
            if k == "P" and e == "P":
                continue
            if known[e].get(k, -1) < p and best.get(k, (-1, 0))[0] < p:
                best[k] = (p, d)
        w = []
        for k, (p, d) in sorted(best.items(), key=lambda z: -z[1][1]):
            if known[e].get(k, -1) >= p:
                continue
            w.append(d)
            need.add(d)
            for k2, p2 in clock[d].items():
                known[e][k2] = max(known[e].get(k2, -1), p2)
            known[e][k] = p
        waits.append(w)
        clock.append(dict(known[e]))
        cnt[key] = cnt.get(key, -1) + 1
        pos.append((key, cnt[key]))
        for n, el in rd:
            lastr[n].setdefault(key, np.full(lastw[n].size, -1))[el] = i
        for n, el in wr:
            lastw[n][el] = i
        for n, el in rd + wr:
            if SCRATCH[n][0] == "psum":
                bank.setdefault(n, {})[e] = i
    val, tot = {}, {}
    for i, (e, fn, rd, wr, own) in enumerate(ops):
        for d in waits[i]:
            q[e].wait_ge(T.sem[val[d][0]], val[d][1])
        ins = fn() if fn else None
        if own:
            val[i] = own
            tot[own[0]] = own[1]
            if own[0][0] == "d":
                ins.then_inc(T.sem[own[0]], 16)
        elif i in need:
            tot["c" + e] = tot.get("c" + e, 0) + 1
            val[i] = ("c" + e, tot["c" + e])
            ins.then_inc(T.sem["c" + e], 1)
    for s, n in tot.items():
        g.wait_ge(T.sem[s], n)


def rank_program(g, core, T, topo):
    rank = T.rank_of(core)
    if rank is None:
        return
    ops, nd = [], [0]
    V, S, PE = g.vector, g.scalar, g.tensor

    def v(n, *ix):
        n = SAME.get(n, n)
        ix = ix or (slice(None),) * (len(SHAPES[n]) - 1)
        return (T[n][(slice(None),) + ix], [(n, _IDX[n][ix].ravel())])

    def c(n, a, b=None, st=None):
        return v(n, slice(a, a + 1 if b is None else b, st))

    def ind(w, o):
        return (w[0].indirect(o[0]), w[1], o[1])

    def rec(e, fn, out, ins, own=None):
        rd = []
        for x in ins:
            if isinstance(x, tuple):
                rd += x[1] + (x[2] if len(x) > 2 else [])
        ops.append((e, fn, rd + (out[2] if len(out) > 2 else []), list(out[1]), own))

    def ap(x):
        return x[0] if isinstance(x, tuple) else x

    def cp(o, i):
        rec("V", lambda: V.tensor_copy(o[0], i[0]), o, [i])

    def ms(o, k):
        rec("V", lambda: V.memset(o[0], k), o, [])

    def tt(o, a, b, op):
        rec("V", lambda: V.tensor_tensor(o[0], a[0], b[0], op), o, [a, b])

    def ts(o, a, s1, o0, s2=None, o1=None):
        if o1 is None:
            rec("V", lambda: V.tensor_scalar(o[0], a[0], ap(s1), None, o0), o, [a, s1])
        else:
            rec("V", lambda: V.tensor_scalar(o[0], a[0], ap(s1), ap(s2), o0, o1), o, [a, s1, s2])

    def scan(o, a, b, o0, o1, first=0.0):
        rec("V", lambda: V.tensor_tensor_scan(o[0], a[0], b[0], first, o0, o1), o, [a, b])

    def act(o, i, fu=F.Identity, bias=0.0, scale=1.0):
        rec("S", lambda: S.activation(o[0], i[0], fu, bias=ap(bias), scale=ap(scale)), o, [i, bias, scale])

    def mm(o, l, r, st, sp):
        rec("P", lambda: PE.matmul(o[0], l[0], r[0], st, sp), o, [l, r])

    def iota(o, pat, base=0, cm=0):
        if SCRATCH[o[1][0][0]][2] == i32:
            rec("G", lambda: g.iota(o[0], pat, base, cm), o, [])
        else:
            rec("G", lambda: g.iota(o[0], pat, base, cm, allow_small_or_imprecise_dtypes=True), o, [])

    def dma(e, o, i):
        qq = g.sync if e == "Y" else S
        rec(e, lambda: qq.dma_start(o[0], i[0]), o, [i], ("d%d" % nd[0], 16))
        nd[0] += 1

    def hbm(a):
        return (a, [])

    def send(kind, t, to, src, dsts):
        rid, pid = topo.addr(T.cores[to])[:2]
        m = topo.mask(core, T.cores[to])
        k = len(topo.engines(core, T.cores[to]))
        tr = RemoteDMATransfer(dst_ids=[DstId(rid=rid, pnc=pid)] * len(dsts), dma_engine_mask=m, remote_sem=T.sem["a%s%d" % (kind, t)],
                               srcs=[src[0]], dsts=[d[0] for d in dsts])
        rec("G", lambda: g.remote_dma_fused([tr], local_sem=T.sem["l%s%d" % (kind, t)]), (None, []), [src], ("l%s%d" % (kind, t), k))

    def landed(kind, t, frm, dsts):
        k = len(topo.engines(T.cores[frm], core))
        ops.append(("G", None, [], [x for d in dsts for x in d[1]], ("a%s%d" % (kind, t), k * len(dsts))))

    def sel(n0, n1, r):
        return c(n0, 15 - r, 143 - r) if r % 2 else c(n1, 16 - r, 144 - r)

    def keys(out, buf, a, n):
        for r in range(16):
            mm(out, sel("W0", "W1", r), c(buf, a + r, a + 16 * n, 16), r == 0, r == 15)

    add, sub, mul, mx, mn = A.add, A.subtract, A.mult, A.max, A.min
    shr, band = A.arith_shift_right, A.bitwise_and

    dma("Y", v("SE"), hbm(T["seat"][:]))
    dma("Y", v("WI"), hbm(T["wt"][:]))
    dma("S", v("PU"), hbm(T["pup"][:]))
    dma("S", c("D", 0, 4096), hbm(T["dic"][:, 0:4096]))
    dma("Y", c("D", 4096, 8192), hbm(T["dic"][:, 4096:8192]))
    dma("Y", c("D", 8192, 8496), hbm(T["dic"][:, 0:304]))

    iota(c("CI", 0), [[0, 1]], 0, 1)
    iota(c("IO", 0, 144), [[1, 144]])
    iota(c("T2", 0, 128), [[16, 8], [0, 16]])
    iota(c("T2", 128, 256), [[-1, 16], [0, 8]], 15)
    iota(c("T2", 256, 264), [[92, 2], [-4, 4]], 45)
    iota(c("T2", 264, 272), [[2, 2], [0, 4]], 1)
    iota(c("T2", 272, 280), [[0, 2], [16, 4]], 7)
    iota(v("DMC"), [[16, 8], [0, 8]], DUM)
    iota(v("DL"), [[128, 2], [16, 8]], LAND)
    iota(v("ONE"), [[0, 512]], 1)
    iota(v("FL"), [[0, 1024]], 1)
    iota(c("IO", 144, 1024), [[1, 880]], 144)
    iota(v("KC"), [[0, 16], [8, 8]], -4)
    iota(v("KD"), [[0, 4], [8, 16]], -4)
    iota(v("TB"), [[0, 560]], 0)
    iota(v("J16"), [[0, 8], [-16, 8]], 112)
    iota(v("J37"), [[0, 8], [-37, 8]], 259)
    iota(v("KM"), [[0, 72]], -1024)
    iota(v("RB"), [[0, 64]], 0)
    iota(v("CC"), [[0, 72]], 0)
    iota(v("CD"), [[0, 128]], 0)
    for n in ("X0", "X1"):
        iota(c(n, DUM, NEG), [[0, 128]], 0)
        iota(c(n, NEG, LAND), [[0, 16]], -1)
    iota(c("LT", 0, 1024), [[0, 1024]], 0)
    iota(v("BIG"), [[0, 1024]], 2048)
    cR, c64, cK, cE, c7, cG, cP, cW, cG15, cG16, cP1, cN15, cX, c8 = [c("CF", i) for i in range(14)]
    y = [c("CF", i) for i in range(14, 30)]
    cOdd, cEven = c("CF", 30), c("CF", 31)
    ts(c("CI", 1), c("CI", 0), 15, band)
    ts(c("CI", 2), c("CI", 0), 7, band)
    ts(c("CI", 3), c("CI", 0), 3, shr, 1, band)
    ts(c("CI", 4), c("CI", 0), 112, band)
    cp(cR, c("CI", 1)); cp(cK, c("CI", 2)); cp(cE, c("CI", 3)); cp(cG, c("CI", 4)); cp(cP, c("CI", 0))
    ts(c64, cR, 64.0, mul, -1.0, add)
    ts(c8, cR, 8.0, mul)
    ts(c7, cK, 7.0, A.is_equal)
    ts(cG15, cG, 15.0, add); ts(cG16, cG, 16.0, add); ts(cP1, cP, 1.0, add); ts(cN15, cR, 15.0, A.not_equal)
    ts(c("TI", 0, 74), c("IO", 0, 74), c64, add)
    ts(v("C0"), c("IO", 0, 144), cG15, A.is_equal); ts(v("C1"), c("IO", 0, 144), cG16, A.is_equal)
    ts(c("TI", 80, 154), c("TI", 0, 74), 1023, band)
    ts(v("ID"), c("IO", 0, 128), cP, A.is_equal); ts(v("NI"), c("IO", 0, 128), cP, A.is_equal, -1.0, mul)
    cp(v("PIL"), c("TI", 80, 154))
    ts(y[0], cE, 2.0, mul); ts(y[1], c7, 23.0, mul, 23.0, add); ts(y[2], c7, -168.0, mul, 206.0, add); ts(y[3], cE, 8.0, mul)
    ts(y[4], c7, -122.0, mul, 252.0, add); ts(y[5], c7, -8.0, mul, 408.0, add); ts(y[6], cE, -1.0, mul, 1.0, add)
    ts(y[7], cK, -16.0, mul, 127.0, add); ts(y[11], cR, 16.0, add)
    tt(y[8], y[2], cK, sub); tt(y[9], y[4], cK, sub); tt(y[10], y[5], cK, add)
    cp(v("SEU"), v("SE"))
    ts(cX, v("WI"), 2047.5, A.is_ge, -4096.0, mul)
    ms(v("B1"), 0.5); ms(v("LM"), 1.0); ms(v("KP"), 1.0); ms(v("FH"), 1.0)
    tt(cW, v("WI"), cX, add)
    act(c("LG", 512, 1024), ind(v("PU"), c("SEU", 32, 64)))
    cp(c("LG", 0, 512), ind(v("PU"), c("SEU", 0, 32)))
    ts(v("W0"), c("IO", 0, 144), cG15, A.is_equal, cW, mul); ts(v("W1"), c("IO", 0, 144), cG16, A.is_equal, cW, mul)
    act(c("X0", 448, 1168), ind(v("LG"), c("PIL", 28, 73)))
    cp(c("X0", 0, 448), ind(v("LG"), c("PIL", 0, 28)))

    def constants(late):
        if not late:
            ms(c("B1", 0, 80, 16), 2.0 ** 15); ms(c("LM", 12, 184, 46), 0.0); ms(c("LM", 14, 184, 46), -2.0 ** -21)
            ms(c("KP", 0, 128, 8), 0.0); ms(c("FH", 0, 128, 16), 0.0)
            ms(c("EB", 31, 2944, 32), 0.0); ms(c("X1", 0, 16), 0.0); ms(c("X1", 1040, 1168), 0.0)
            ts(v("T1"), c("IO", 0, 72), c64, add, 1022.5, A.is_gt)
            ts(v("SH"), c("IO", 0, 128), cP1, A.is_equal, cN15, mul)
            ts(v("THR"), v("T1"), -8.0, mul, 6.5, add)
            ts(c("CI", 5), c("CI", 0), 1, shr, 7, band); ts(c("CI", 6), c("CI", 0), 1, band)
            cp(y[12], c("CI", 5)); cp(cOdd, c("CI", 6))
            ts(v("MS"), c("IO", 0, 16), y[12], A.is_equal)
            ts(cEven, cOdd, -1.0, mul, 1.0, add)
            ts(c("LS", 54, 62), c("IO", 0, 8), 8.0, mul)
            ts(v("UX"), c("IO", 0, 64), 16.0, mul, y[11], add)
            ts(v("DMC"), v("DMC"), cR, add)
            return
        ts(v("BO"), c("T2", 0, 128), cG, A.is_equal)
        ts(v("MK"), c("T2", 128, 256), cR, A.is_equal)
        tt(v("CR"), v("DMC"), v("UX"), sub)
        ts(v("UA"), v("UX"), -1.0, mul, OFF + 16, add)
        ts(v("NB"), v("UX"), -1.0, mul, float(NEG - 112), add)
        cp(v("DM8"), c("DMC", 0, 64, 8))
        ts(v("DL"), v("DL"), cR, add)
        ts(v("AC"), c("IO", 0, 8), c8, add, 2048.0, mul)
        scan(v("PW"), v("B1"), c("ONE", 0, 80), mul, mul, 4.0)
        ts(c("LS", 0, 8), c("T2", 256, 264), y[0], sub)
        ts(c("LS", 8, 16), c("T2", 264, 272), y[1], mul, y[8], add)
        ts(c("LS", 16, 24), c("T2", 272, 280), y[3], add)
        ts(c("LS", 24, 28), c("IO", 0, 4), 0.0, mul, y[9], add)
        ts(c("LS", 28, 32), c("IO", 0, 4), 0.0, mul, y[10], add)
        ts(c("T2", 280, 281), cK, -2.0, mul, 45.0 - 276, add)
        for b, base in ((1, 287), (2, 424), (3, 488)):
            ts(c("T2", 280 + b), cK, 8.0, mul, float(base - 276), add)
        ms(c("LS", 36), 56)
        ts(c("LS", 37, 41), c("IO", 0, 4), 16.0, mul, 7.0, add)
        ts(c("LS", 42, 46), c("IO", 0, 4), 2.0, mul, cE, add)
        ts(y[13], y[3], 7.0, add)
        ts(c("LS", 62, 66), c("IO", 0, 4), 16.0, mul, y[13], add)
        ts(c("LS", 46, 54), c("IO", 0, 8), 0.0, mul, y[7], add)
        ts(c("LS", 32, 36), c("T2", 280, 284), y[6], mul, 276.0, add)
        for b in range(4):
            ms(c("EB", 736 * b + 15, 736 * b + 224, 32), -8.0)
            ts(c("EB", 736 * b + 239, 736 * b + 736, 32), c("PW", 0, 16), 2.0 ** -19, mul)
        ms(c("FL", 1, 1024, 16), 0.0)

    def halo(n, e, left):
        f = cp if e == "V" else act
        if left:
            f(c(n, 0, 16), c(n, 1023, 1039))
        else:
            f(c(n, 1040, 1168), c(n, 17, 145))

    constants(0)
    for t in range(RO):
        X, Xn, O, On = ("X0", "X1", "O0", "O1") if t % 2 == 0 else ("X1", "X0", "O1", "O0")
        host, guest = (rank + 1 + t % (N - 1)) % N, (rank - 1 - t % (N - 1)) % N
        land = LAND + 128 * (t // 2)
        dl = c("DL", 8 * (t // 2), 8 * (t // 2) + 8)
        rcv, vl, rl = c("RCV", 128 * t, 128 * t + 128), c("VL", 128 * t, 128 * t + 128), c("RL", 128 * t, 128 * t + 128)
        landed("k", t, guest, [rcv]); landed("v", t, guest, [vl, c(Xn, land, land + 128)]); landed("r", t, host, [rl])

        keys(c("PK", 0, 72), X, 16, 72)
        ts(v("K0"), c("PK", 0, 72), 524288.0, add)
        ts(v("KI"), v("K0"), 4095, band)

        def n1(j):
            tt(c("PR", 64 * j, 64 * j + 64), c("PV" if j != 3 else "KI", 0, 64), c("KI", j, j + 64), mul)

        def n2(a, b):
            ts(c("PS", 64 * a, 64 * b), c("PR", 64 * a, 64 * b), 5, shr, 8191, band)

        def n3(j):
            ts(c("IX", 64 * j, 64 * j + 64), c("PS", 64 * j, 64 * j + 64), float(37 * j + 11 * t), add)

        def xs(u):
            a = 16 + 16 * (u // 2) + 512 * (u % 2)
            return c(X, a, a + 512)

        def lt(u, n=1):
            return c("LT", 1024 + 512 * u, 1024 + 512 * (u + n))

        def sg(u):
            k = (u % 6 + u // 6 * 2) % 3
            z = v("PZ%d" % k)
            mm(z, v("NI"), xs(u), True, False)
            act(c("DG", 512 * k, 512 * k + 512), ind(v("D"), c("IX", 32 * u, 32 * u + 32)))
            mm(z, v("ID"), c("DG", 512 * k, 512 * k + 512), False, True)

        def ss(u):
            act(lt(u), v("PZ%d" % ((u % 6 + u // 6 * 2) % 3)), F.Sigmoid, -128.0, 256.0)

        def vg(u, n):
            a = 16 + 16 * (u // 2) + 512 * (u % 2)
            tt(lt(u, n), ind(v("D"), c("IX", 32 * u, 32 * (u + n))), c(X, a, a + 512 * n), A.is_gt)

        def cnt(j):
            return c({3: "PC", 4: "PA", 0: "PB", 5: "PC", 1: "PA", 6: "PC", 7: "PB", 2: "PA"}[j], 64 * j, 64 * j + 64)

        def count(j):
            for r in range(16):
                mm(cnt(j), sel("C0", "C1", r), c("LT", 1024 * (j + 1) + r, 1024 * (j + 2), 16), r == 0, r == 15)

        def missed(j):
            if j == 0:
                ts(c("FL", 15, 1024, 16), cnt(0), 6.5, A.is_ge, -1.0, mul)
            else:
                tt(v("F7") if j == 7 else c("FL", 15 - 2 * j, 1024, 16), cnt(j), c("THR", j, j + 64), A.is_ge)

        n1(3)
        cp(c("PV", 0, 64), c("KI", 0, 64))
        n2(3, 4); n1(0); n3(3); n1(4); n2(0, 1); n1(1); n1(2); n3(0); n2(4, 5)
        if t == 0:
            constants(1)
        sg(6); sg(0); ss(6)
        vg(7, 1)
        n3(4); n2(1, 3); n1(5); n1(6); n1(7); n3(1); n3(2)
        vg(8, 2)
        n2(5, 8)
        ts(v("S1"), c("KI", 0, 64), 2048.0, mul)
        n3(5); n3(6); n3(7)
        tt(c("C3", 0, 64), v("S1"), v("CR"), add)
        count(3); sg(1); ss(0); count(4); sg(2); ss(1); count(0)
        vg(10, 2); missed(3); missed(4); sg(3); ss(2); count(5)
        vg(12, 2); missed(0); missed(5); sg(4); count(6); ss(3); count(1); sg(5); ss(4)
        vg(14, 2); missed(1); missed(6); count(7); ss(5); count(2)
        if t > 0:
            halo(X, "V", True)
        ts(c("K0", 0, 64), c("PR", 0, 64), 1, shr, 16368, band)
        missed(7); missed(2)
        if t == 0:
            act(c("O1", 0, 1024), ind(v("IO"), v("SEU")))
            act(v("O0"), ind(c("O1", 0, 1024), c("PIL", 0, 73)))

        un, tmp, a2, bb = c("PV", 64, 128), c("PV", 128, 192), c("PV", 320, 392), c("PV", 392, 456)

        def lengths(h):
            return lambda: scan(c("JS", 128 * h, 128 * h + 128), c("ONE", 0, 128), c("FL", 256 * h + 1, 256 * h + 256, 2), add, mul)

        def halo_starts():
            tt(c("A2", 0, 8), c("PV", 184, 192), c("UA", 56, 64), add)

        def moves():
            act(v("S1"), c("JS", 7, 512, 8), scale=-16.0)
            tt(v("S2"), v("NB"), un, mul)

        fill = [lengths(0), lengths(1), lengths(2), lengths(3),
                lambda: tt(v("S1"), c("JS", 7, 512, 8), v("F7"), mul),
                lambda: ts(un, v("S1"), -6.5, A.is_le),
                lambda: ts(tmp, v("S1"), -6.5, A.is_le, 7168.0, mul),
                halo_starts,
                moves,
                lambda: tt(c("PV", 328, 392), tmp, v("UA"), add),
                lambda: tt(c("PV", 192, 256), c("C3", 0, 64), un, mul),
                lambda: tt(c("PV", 256, 320), c("K0", 0, 64), un, mul),
                lambda: tt(bb, v("S1"), v("S2"), add),
                lambda: tt(c("FT", 0, 56), c("WT", 0, 56), c("WT", 1, 57), sub)]
        for p in range(15, -1, -1):
            for b in range(4):
                a, f0 = 736 * b + 32 * (22 - p), 16 * (16 * b + p)
                scan(c("EB", a + 18, a + 32), c("EB", a - 209, a, 16), c("FL", f0 + 2, f0 + 16), add, mul)
        tt(c("TB", 184, 276), c("EB", 15, 2944, 32), c("EB", 31, 2944, 32), add)
        scan(c("TB", 0, 184), v("LM"), c("EB", 15, 2944, 16), mul, add)
        fill.pop(0)()
        tt(v("M1"), ind(c("TB", 0, 184), c("LS", 0, 8)), v("KC"), A.is_lt)
        act(v("E1"), ind(c("TB", 0, 280), c("LS", 8, 16)))
        fill.pop(0)()
        scan(c("TB", 280, 408), v("M1"), v("E1"), mul, add)
        fill.pop(0)()
        tt(c("TB", 408, 415), c("TB", 351, 407, 8), c("TB", 359, 415, 8), sub)
        act(v("E1"), ind(c("TB", 0, 416), c("LS", 24, 32)))
        tt(v("M1"), ind(c("TB", 280, 344), c("LS", 16, 24)), v("KC"), A.is_lt)
        fill.pop(0)()
        scan(c("TB", 417, 545), v("M1"), v("E1"), mul, add)
        fill.pop(0)()
        tw = c("TB", 488, 552)
        cp(c("U", 0, 8), c("TB", 488, 552, 8))
        act(v("E1"), ind(tw, c("LS", 54, 62)), scale=cEven)
        fill.pop(0)()
        cp(c("PR", 0, 128), ind(tw, c("U", 0, 8)))
        act(v("M1"), ind(tw, c("U", 0, 8)), scale=cOdd)
        fill.pop(0)()
        ts(c("U", 8), c("PR", 0), 2.0, mul, 2.0, add)
        tt(v("F2"), v("E1"), v("M1"), add)
        act(c("G", 0, 2), c("F2", 0, 2), scale=c("MS", 0))
        mm(c("PB", 0, 2), v("SH"), c("G", 0, 2), True, False)
        act(v("WT"), ind(c("TB", 0, 552), c("LS", 32, 36)))
        for s in range(1, 8):
            li = c("U", 8) if s == 1 else c("U", 32 * (s - 1) + 2 * (2 * s - 3))
            if s < 7:
                ts(c("U", 32 * s, 32 * s + 32, 2), ind(c("PR", 0, 128), li), 2.0, mul, 2.0 * s + 2, add)
                act(c("G", 16 * s, 16 * s + 16), ind(v("F2"), li), scale=c("MS", s))
            else:
                ts(c("G", 16 * s, 16 * s + 16), ind(v("F2"), li), c("MS", s), mul)
            mm(c("PB", 0, 2), v("SH"), c("G", 18 * s - 1, 18 * s + 1), False, s == 7)
            fill.pop(0)()
        mm(c("PA", 0, 8), v("SH"), c("A2", 0, 8), True, True)
        while fill:
            fill.pop(0)()
        ts(c("M1", 0, 56), c("KD", 0, 56), c("PB", 0), A.is_gt)
        cp(c("RB", 56), c("PB", 0))
        scan(c("RB", 0, 56), c("M1", 0, 56), c("FT", 0, 56), mul, add)
        tt(v("B1"), ind(v("RB"), c("LS", 36, 41)), v("PW"), mul)
        cp(c("PV", 320, 328), c("PA", 0, 8))
        ts(v("B2"), v("B1"), -0.5, add)
        ts(v("ST"), v("B2"), 1, band)
        st = c("ST", 16, 80)
        tt(c("P3", 0, 64), st, c("PV", 192, 256), mul)
        tt(c("P3", 64, 128), st, c("PV", 256, 320), mul)
        tt(v("P1"), c("ST", 8, 80), a2, mul)
        tt(v("P2"), st, bb, mul)
        snd = c("SND", 128 * t, 128 * t + 128)
        scan(snd, v("KP"), v("P3"), mul, add)
        scan(v("YS"), v("KM"), v("P1"), add, mx)
        send("k", t, host, snd, [rcv])
        tt(v("A2", slice(8, 72)), v("P2"), v("UX"), add)
        ts(v("NL"), c("YS", 8, 72), -1.0, mul, OFF, add)
        ts(tmp, c("YS", 8, 72), OFF - 1023.5, A.is_le, -16.0, mul)
        cp(v("HA"), c("SND", 128 * t + 7, 128 * t + 64, 8))
        tt(v("SR"), v("A2", slice(8, 72)), tmp, add)
        ts(v("AI"), v("HA"), 2047, band)
        cp(v("SL"), v("SR"))
        tt(v("AF"), v("DM8"), v("AI"), sub)
        for h in range(4):
            act(c("LG", 256 * h, 256 * h + 256), ind(v("LT"), c("NL", 16 * h, 16 * h + 16)))
        for h in range(4):
            tt(c(Xn, 16 + 256 * h, 272 + 256 * h), ind(c(X, 0, LAND), c("SL", 16 * h, 16 * h + 16)), c("LG", 256 * h, 256 * h + 256), add)
            if h == 0:
                cp(v("AWL"), v("AF"))
        vs = c("VS", 128 * t, 128 * t + 128)
        act(vs, ind(c(X, 0, NEG), v("AWL")))
        send("v", t, host, vs, [vl, c(Xn, land, land + 128)])

        def seats():
            ts(v("S1"), v("SR"), NEG - 0.5, A.is_ge)
            ts(v("S2"), v("UX"), float(-NEG), add)
            tt(v("UN"), v("S1"), v("S2"), mul)
            tt(v("BB"), v("UN"), v("SR"), add)
            cp(v("OL"), v("BB"))
            act(c(On, 16, 1040) if t < RO - 1 else v("OH"), ind(v(O), v("OL")))

        got = c("RCV", 128 * t + 7, 128 * t + 64, 8)
        tt(v("RAW"), ind(c("RCV", 128 * t + 64, 128 * t + 128), c("LS", 62, 66)), v("J16"), add)
        ts(v("HS"), got, 1.0 / 2048, mul, 2.0 ** -12 - 0.5, add)
        ts(v("H1"), v("RAW"), 1008, band)
        ts(v("K4"), v("RAW"), 10, shr, 15, band)
        ts(v("HV"), got, 0.5, A.is_ge, 6.5, mul)
        tt(c("CC", 0, 64), v("H1"), v("K4"), add)
        cp(v("VLS"), c("CC", 0, 64))
        act(c("XV", 512, 1024), ind(c(Xn, 16, 1040), c("VLS", 32, 64)))
        cp(c("XV", 0, 512), ind(c(Xn, 16, 1040), c("VLS", 0, 32)))
        keys(c("PK", 0, 64), "XV", 0, 64)
        if t == RO - 1:
            seats()
            for r in range(16):
                mm(c("PV", 0, 64), sel("C0", "C1", r), c("OH", r, 1024, 16), r == 0, r == 15)
        cp(v("THV"), ind(v("HV"), c("LS", 42, 46)))
        if t == 0:
            cp(c("PK", 128, 192), v("J37"))
        tt(c("CD", 1, 128, 2), c("CC", 0, 64), c("CC", 1, 65), sub)
        ts(v("HC"), c("CC", 0, 64, 8), 16.0, add)
        ts(c("CD", 15, 128, 16), c("CC", 7, 64, 8), 16.0, add)
        tt(c("CD", 0, 128, 16), dl, v("HC"), sub)
        ts(v("K2"), c("PK", 0, 64), 524288.0, add)
        ts(v("K3"), v("K2"), 4095, band)
        tt(v("K4"), ind(v("HS"), c("LS", 42, 46)), v("K3"), mul)
        ts(v("K2"), v("K4"), 5, shr, 8191, band)
        tt(v("K3"), v("K2"), c("PK", 128, 192), add)
        ts(v("IX2"), v("K3"), float(11 * t), add)
        mm(c("PZ0", 0, 256), v("NI"), c("XV", 768, 1024), True, False)
        act(c("DG", 0, 256), ind(v("D"), c("IX2", 48, 64)))
        mm(c("PZ0", 0, 256), v("ID"), c("DG", 0, 256), False, True)
        act(c("L2", 768, 1024), c("PZ0", 0, 256), F.Sigmoid, -128.0, 256.0)
        tt(c("L2", 0, 768), ind(v("D"), c("IX2", 0, 48)), c("XV", 0, 768), A.is_gt)
        for r in range(16):
            mm(c("PC", 0, 64), sel("C0", "C1", r), c("L2", r, 1024, 16), r == 0, r == 15)
        if t == RO - 1:
            ts(v("OF"), c("PV", 0, 64), 1.0 / 16, mul)
            ts(v("OL"), c("PV", 0, 64), 1.0 / 16, mul)
            ts(v("S2"), c("P3", 0, 64), 0.5, A.is_ge)
            tt(v("S1"), v("OF"), v("DMC"), sub)
            dma("Y", hbm(T["yseat"][:]), v("OF"))
            tt(v("UN"), v("S1"), v("S2"), mul)
            scan(v("BB"), c("KP", 0, 64), v("UN"), mul, add)
        tt(c("FH", 1, 128, 2), c("PC", 0, 64), v("THV"), A.is_ge)
        scan(v("CH"), v("FH"), v("CD"), mul, add)
        tt(v("ME"), ind(v("CH"), c("LS", 46, 54)), v("MK"), mul)
        ts(v("NCH"), c("CH", 15, 128, 16), -1024.0, mul)
        mm(c("PB", 0, 128), v("BO"), v("ME"), True, True)
        mm(c("PA", 0, 128), v("BO"), v("ME"), True, True)
        tt(v("CRL"), c("CH", 15, 128, 16), v("AC"), add)
        nv = 3
        if t == RO - 1:
            tt(v("AF"), c("BB", 7, 64, 8), v("DM8"), add)
        for k in range(8):
            if k < nv:
                ts(c("NQ", 128 * k, 128 * k + 128), c("PA", 0, 128), c("CH", 16 * k + 15), A.not_equal, 524288.0, mul)
            else:
                act(c("NQ", 128 * k, 128 * k + 128), c("PB", 0, 128), F.Square, c("NCH", k), 1024.0)
        scan(c("FM", 0, 384), c("BIG", 0, 384), c("NQ", 0, 384), add, mn)
        scan(c("FM", 384, 1024), c("BIG", 384, 1024), c("NQ", 384, 1024), add, mn)
        tt(v("WN"), v("CRL"), c("FM", 127, 1024, 128), sub)
        tt(v("NCH"), v("WN"), dl, mn)
        cp(v("CHL"), v("NCH"))
        rs = c("RS", 128 * t, 128 * t + 128)
        cw = c(Xn, 0, land + 128)
        cp(rs, ind(cw, v("CHL")))
        send("r", t, guest, rs, [rl])
        cp(ind(cw, v("CHL")), vl)
        if t < RO - 1:
            seats()
            halo(On, "S", False); halo(On, "S", True)
            cp(ind(c(Xn, 0, NEG), v("AWL")), rl)
            halo(Xn, "V", False)
        else:
            cp(v("OA"), v("AF"))
            cp(ind(c("Y", 0, 1024), v("OL")), c(Xn, 16, 1040))
            cp(ind(v("Y"), v("OA")), rl)
            dma("Y", hbm(T["ypup"][:, 0:512]), c("Y", 0, 512))
            dma("S", hbm(T["ypup"][:, 512:1024]), c("Y", 512, 1024))
    order_calls(g, T, ops)
